import numpy as np
import ml_dtypes


def mxq(x, axis, fmt="e4m3"):
    dtype, down = {"e4m3": (ml_dtypes.float8_e4m3fn, 7), "e5m2": (ml_dtypes.float8_e5m2, 14)}[fmt]
    v = np.moveaxis(np.asarray(x, np.float32).astype(ml_dtypes.bfloat16).astype(np.float64), axis, -1)
    blocks = v.reshape(v.shape[:-1] + (-1, 32))
    amax = np.abs(blocks).max(-1, keepdims=True)
    byte = np.maximum(np.where(amax > 0, np.frexp(amax)[1] - 1 + 127, 0) - down, 1)
    scale = np.exp2(byte - 127.0)
    codes = (blocks / scale).astype(np.float32).astype(dtype).astype(np.float64)
    return np.moveaxis((codes * scale).reshape(v.shape), -1, axis)


WIDE = False


def mx_kscale(k):
    if not WIDE:
        return np.ones(k)
    levels = np.array([10, -10, 5, -5, 0])
    if k % 512:
        return np.exp2(np.random.permutation(np.resize(levels, k // 32))).repeat(32)
    a = np.empty((k // 512, 16))
    for p in range(k // 512):
        a[p, :8] = np.random.permutation(np.resize(levels, 8))
        for g in range(8):
            far = levels[np.abs(levels - a[p, g]) >= 10]
            a[p, g + 8] = far[np.random.randint(len(far))]
    return np.exp2(a.ravel()).repeat(32)


def f64(x):
    return np.asarray(x).astype(np.float64)


def striped(idx):
    return np.tile(idx.reshape(-1, 16).T, (8, 1)).astype(np.uint16)


def unstriped(offs):
    return offs[:16].T.reshape(-1).astype(np.int64)


E2M1 = np.array([0.0, 0.5, 1.0, 1.5, 2.0, 3.0, 4.0, 6.0, -0.0, -0.5, -1.0, -1.5, -2.0, -3.0, -4.0, -6.0])


def pack_weight(w, fmt):
    k, n = w.shape
    w = f64(np.asarray(w, np.float32).astype(ml_dtypes.bfloat16)).reshape(k // 32, 32, n)
    amax = np.abs(w).max(1)
    if fmt == "e4m3":
        byte = np.frexp(amax)[1] - 1 + 127 - 7
    else:
        mant, ex = np.frexp(amax / 6.0)
        byte = np.where(mant > 0.5, ex, ex - 1) + 127
    byte = np.clip(np.where(amax > 0, byte, 1), 1, 254)
    scaled = (w * np.exp2(127.0 - byte)[:, None, :]).reshape(k, n).astype(np.float32)
    by_word = np.ascontiguousarray(scaled.reshape(k // 512, 128, 4, n).transpose(0, 1, 3, 2))
    if fmt == "e4m3":
        words = by_word.astype(ml_dtypes.float8_e4m3fn).view(np.uint8)
    else:
        c = by_word.astype(ml_dtypes.float4_e2m1fn).view(np.uint8) & 0xF
        words = (c[..., 0::2] | (c[..., 1::2] << 4)).reshape(k // 512, 128, 2 * n)
    return np.ascontiguousarray(words), np.ascontiguousarray(byte.astype(np.uint8).reshape(k // 512, 16, n))


def unpack_weight(words, scales, fmt):
    g, _, n = scales.shape
    words = np.ascontiguousarray(words).reshape(g, 128, n, -1)
    if fmt == "e4m3":
        vals = words.view(ml_dtypes.float8_e4m3fn).astype(np.float64)
    else:
        nib = np.empty((g, 128, n, 4), np.uint8)
        nib[..., 0::2] = words & 0xF
        nib[..., 1::2] = words >> 4
        vals = E2M1[nib]
    vals = vals * np.repeat(np.exp2(scales.astype(np.float64) - 127.0), 8, axis=1)[..., None]
    return vals.transpose(0, 1, 3, 2).reshape(g * 512, n)


def gelu(v):
    return 0.5 * v * (1.0 + np.tanh(np.sqrt(2.0 / np.pi) * (v + 0.044715 * v**3)))


def striped8(idx):
    return np.concatenate([v.reshape(-1, 16).T for v in idx]).astype(np.uint16)


def unstriped8(offs):
    return np.stack([offs[16 * g:16 * g + 16].T.reshape(-1) for g in range(8)]).astype(np.int64)


def heads(h, wgt, idx8):
    r = np.arange(h.shape[0])
    return wgt[r // 4 % 128] * h[r[:, None], idx8[r % 512 // 64]]


def put_heads(h, wgs, idx8, t2):
    r = np.arange(h.shape[0])
    page = np.zeros((h.shape[0], t2))
    page[r[:, None], idx8[r % 512 // 64]] = wgs[r // 4 % 128] * h
    return page


K, H, T, S, P, T2 = 1536, 1024, 2048, 1024, 512, 1024

def setup_inputs():
    n = np.random.standard_normal
    s = mx_kscale(K)[:, None]
    u = mx_kscale(H)[:, None]
    d = {}
    d["tab_words"], d["tab_scales"] = pack_weight(n((K, T)) * s, "e4m3")
    d["w4_words"], d["w4_scales"] = pack_weight(n((K, H)) / K**0.5 / s * u.T, "e2m1")
    d["w2"] = (n((H, H)) / H**0.5 / u / u.T).astype(np.float32)
    d["metal"] = (0.9 * n(H) * u[:, 0]).astype(np.float32)
    d["prior"] = (1.2 * n((H, P))).astype(np.float32)
    d["wgt"] = np.repeat(np.random.uniform(0.5, 2.0, (8, P)), 16, axis=0).astype(np.float32)
    d["wgo"] = np.repeat(np.random.uniform(0.5, 2.0, (8, P)), 16, axis=0).astype(np.float32)
    d["offs"] = striped(np.random.permutation(T)[:S])
    d["offs2"] = striped8(np.stack([np.random.permutation(S)[:P] for _ in range(8)]))
    d["offs3"] = striped8(np.stack([np.random.permutation(T2)[:P] for _ in range(8)]))
    return d

def reference(tab_words, tab_scales, w4_words, w4_scales, w2, metal, prior, wgt, wgo, offs, offs2, offs3):
    v = unpack_weight(tab_words, tab_scales, "e4m3")[:, unstriped(offs)]
    w4 = unpack_weight(w4_words, w4_scales, "e2m1")
    h = w4.T @ v
    x = heads(h, f64(wgt), unstriped8(offs2))
    z = x + f64(metal)[:, None]
    e = mxq(f64(w2), 0, "e4m3").T @ mxq(z, 0, "e4m3")
    y = e * x + f64(prior)
    return put_heads(y, f64(wgo), unstriped8(offs3), T2)

@@ -1,0 +1,293 @@
+from contextlib import ExitStack
+
+import concourse.mybir as mybir
+from concourse.masks import make_identity
+
+K, H, T, S, M, T2 = 1536, 1024, 2048, 1024, 512, 1024
+FLOPS = 2 * K * H * S + 2 * H * H * M
+
+F32 = mybir.dt.float32
+BF16 = mybir.dt.bfloat16
+I32 = mybir.dt.int32
+U32 = mybir.dt.uint32
+U16 = mybir.dt.uint16
+U8 = mybir.dt.uint8
+FP8X4 = mybir.dt.float8_e4m3fn_x4
+FP4X4 = mybir.dt.float4_e2m1fn_x4
+MULT = mybir.AluOpType.mult
+ADD = mybir.AluOpType.add
+IDENTITY = mybir.ActivationFunctionType.Identity
+
+P = 128
+PACK = 4
+N = 512
+PASSES1 = K // (P * PACK)
+PASSES2 = H // (P * PACK)
+TILES = H // P
+HALVES = S // N
+PAGES = 3
+
+
+def tile_list_jewellery_drawer_appraisal_kernel(
+    tc, tab_words, tab_scales, w4_words, w4_scales, w2, metal, prior, wgt, wgo, offs, offs2, offs3, out
+):
+    nc = tc.nc
+
+    def rows(dram, j):
+        b, i = divmod(j, PACK)
+        return dram.rearrange("(b u i s) c -> b i u s c", b=PASSES2, i=PACK, s=8)[b, i]
+
+    with ExitStack() as ctx:
+        keep = ctx.enter_context(tc.tile_pool(name="keep", bufs=1))
+        ring = ctx.enter_context(tc.tile_pool(name="ring", bufs=2))
+        hpool = ctx.enter_context(tc.tile_pool(name="hpool", bufs=4))
+        psum = ctx.enter_context(tc.psum_pool(name="psum", bufs=8))
+
+        list1 = keep.tile([P, S // 16], U16, name="list1")
+        list2 = keep.tile([P, M // 16], U16, name="list2")
+        list3 = keep.tile([P, M // 16], U16, name="list3")
+        tscale = keep.tile([P, T], U8, name="tscale", align_bytes=64)
+        wscale_raw = keep.tile([P, PASSES1, H], U8, name="wscale_raw", align_bytes=64)
+        vscale = [keep.tile([P, S], U8, name=f"vscale{a}", align_bytes=64) for a in range(PASSES1)]
+        pages = [keep.tile([P, T2], F32, name=f"page{g}") for g in range(PAGES)]
+        metal_rows = keep.tile([P, P], F32, name="metal_rows")
+        ident = keep.tile([P, P], F32, name="ident")
+
+        nc.vector.memset(tscale[:].bitcast(I32), 0)
+        nc.vector.memset(wscale_raw[:].bitcast(I32), 0)
+        for a in range(1, PASSES1):
+            nc.vector.memset(vscale[a][:].bitcast(I32), 0)
+        for page in pages:
+            nc.vector.memset(page[:], 0.0)
+        nc.gpsimd.memset(metal_rows[:], 0.0)
+        make_identity(nc, ident[:])
+
+        nc.sync.dma_start(list1[:], offs)
+        for q in range(4):
+            queue = nc.sync if q < 2 else nc.scalar
+            queue.dma_start(
+                tscale[32 * q : 32 * q + 4 * PASSES1, :].bitcast(I32),
+                tab_scales[:, 4 * q : 4 * q + 4, :].bitcast(I32),
+            )
+
+        twords = [keep.tile([P, T], I32, name=f"twords{a}") for a in range(PASSES1)]
+        wwords_raw = keep.tile([P, PASSES1, H // 2], I32, name="wwords_raw")
+
+        def load_table(a):
+            nc.sync.dma_start(twords[a][:], tab_words[a].rearrange("p t i -> p (t i)").bitcast(I32))
+
+        load_table(0)
+        nc.sync.dma_start(wwords_raw[:], w4_words.rearrange("a p n -> p a n").bitcast(I32))
+        for q in range(4):
+            nc.scalar.dma_start(
+                wscale_raw[32 * q : 32 * q + 4, :, :].bitcast(I32),
+                w4_scales[:, 4 * q : 4 * q + 4, :].rearrange("a r n -> r a n").bitcast(I32),
+            )
+        load_table(1)
+        for b in range(PASSES2):
+            nc.scalar.dma_start(
+                metal_rows[PACK * b : PACK * (b + 1), :].rearrange("i (u s) -> i u s", s=8),
+                metal.rearrange("(b u i s) -> b i u s", b=PASSES2, i=PACK, s=8)[b],
+            )
+        metal_bank = psum.tile([P, P], F32, name="bank")
+        nc.tensor.transpose(metal_bank[:], metal_rows[:], ident[:])
+        metal_sb = keep.tile([P, TILES], F32, name="metal_sb")
+        nc.scalar.activation(metal_sb[:], metal_bank[:, 0:TILES], IDENTITY)
+
+        nc.vector.tensor_copy(vscale[0][:], tscale[:].indirect(list1[:]))
+        for a in range(1, PASSES1):
+            nc.scalar.dma_start(vscale[a][0:112, :].bitcast(I32), vscale[0][4 * a : 4 * a + 112, :].bitcast(I32))
+        load_table(2)
+
+        nc.sync.dma_start(list2[:], offs2)
+        wgt_sb = keep.tile([P, M], F32, name="wgt_sb")
+        nc.sync.dma_start(wgt_sb[:], wgt)
+        w2_raw = [keep.tile([P, PACK, H], F32, name=f"w2raw{b}") for b in range(PASSES2)]
+        for j in range(TILES):
+            nc.sync.dma_start(w2_raw[j // PACK][:, j % PACK, :], rows(w2, j))
+        prior_sb = [keep.tile([P, M], F32, name=f"prior{j}") for j in range(TILES)]
+        wgo_sb = keep.tile([P, M], F32, name="wgo_sb")
+        nc.sync.dma_start(list3[:], offs3)
+        nc.sync.dma_start(wgo_sb[:], wgo)
+        for j in range(TILES):
+            nc.sync.dma_start(prior_sb[j][:], rows(prior, j))
+
+        vwords = [[keep.tile([P, N], U32, name=f"vwords{a}_{h}", align_bytes=64) for h in range(HALVES)] for a in range(PASSES1)]
+
+        def gather_table(a):
+            for h in range(HALVES):
+                cols = list1[:, h * (N // 16) : (h + 1) * (N // 16)]
+                nc.vector.tensor_copy(vwords[a][h][:], twords[a][:].bitcast(U32).indirect(cols))
+
+        wwords = [keep.tile([P, PASSES1, PACK, 2 * P], U8, name=f"wwords{b}", align_bytes=64) for b in range(PASSES2)]
+        wscale = [keep.tile([P, PASSES1, PACK, P], U8, name=f"wscale{b}", align_bytes=64) for b in range(PASSES2)]
+
+        def deal_w4(b):
+            nc.vector.tensor_copy(
+                wwords[b][:].bitcast(I32).rearrange("p a i (u w) -> p a i u w", w=4),
+                wwords_raw[:].rearrange("p a (b u i w) -> p b a i u w", b=PASSES2, i=PACK, w=4)[:, b],
+            )
+            nc.vector.tensor_copy(
+                wscale[b][:].bitcast(I32).rearrange("p a i (u w) -> p a i u w", w=2),
+                wscale_raw[:].bitcast(I32).rearrange("p a (b u i w) -> p b a i u w", b=PASSES2, i=PACK, w=2)[:, b],
+            )
+
+        gather_table(0)
+        deal_w4(0)
+        deal_w4(1)
+        gather_table(1)
+        gather_table(2)
+
+        h_sb = {}
+        h_bank = {}
+
+        def first_product(j, h, a):
+            b, i = divmod(j, PACK)
+            if a == 0:
+                h_bank[j, h] = psum.tile([P, N], F32, name="bank")
+            nc.tensor.matmul_mx(
+                out=h_bank[j, h][:],
+                lhsT=wwords[b][:, a, i, :].bitcast(FP4X4),
+                lhsT_scale=wscale[b][:, a, i, :],
+                rhs=vwords[a][h][:].bitcast(FP8X4),
+                rhs_scale=vscale[a][:, h * N : (h + 1) * N],
+                start=(a == 0),
+                stop=(a == PASSES1 - 1),
+            )
+            if a == PASSES1 - 1:
+                if h == 0:
+                    h_sb[j] = hpool.tile([P, S], F32, name="h_sb")
+                nc.scalar.copy(h_sb[j][:, h * N : (h + 1) * N], h_bank[j, h][:])
+
+        x_sb = [keep.tile([P, M], F32, name=f"x{j}") for j in range(TILES)]
+        z_planes = [ring.tile([P, PACK, M], BF16, name="z_planes") for b in range(PASSES2)]
+        z_codes = [keep.tile([P, M], U32, name=f"zcodes{b}", align_bytes=64) for b in range(PASSES2)]
+        z_scale = [keep.tile([P, M], U8, name=f"zscale{b}", align_bytes=64) for b in range(PASSES2)]
+
+        def read_heads(j):
+            nc.vector.tensor_tensor(x_sb[j][:], h_sb[j][:].indirect(list2[:]), wgt_sb[:], MULT)
+
+        def offset_plane(j):
+            b, i = divmod(j, PACK)
+            nc.scalar.activation(z_planes[b][:, i, :], x_sb[j][:], IDENTITY, bias=metal_sb[:, j : j + 1])
+
+        z_woven = {}
+
+        def weave_z(b):
+            z_woven[b] = ring.tile([P, M, PACK], BF16, name="z_woven", align_bytes=64)
+            nc.vector.tensor_copy(z_woven[b][:], z_planes[b][:].rearrange("p i m -> p m i"))
+
+        def quantise_z(b):
+            nc.vector.quantize_mx(
+                out=z_codes[b][:].bitcast(FP8X4), scales=z_scale[b][:], in_=z_woven[b][:].rearrange("p m i -> p (m i)")
+            )
+
+        w2_woven = {}
+        w2_codes = {}
+        w2_scale = {}
+
+        def round_w2(j):
+            bn, i_n = divmod(j, PACK)
+            w2_woven[j] = ring.tile([P, PASSES2, P, PACK], BF16, name="w2_woven", align_bytes=64)
+            for b in range(PASSES2):
+                nc.scalar.copy(
+                    w2_woven[j][:, b].rearrange("p (u s) i -> p u s i", s=8),
+                    w2_raw[b][:].rearrange("p i (c u n s) -> p c n u s i", c=PASSES2, n=PACK, s=8)[:, bn, i_n],
+                )
+
+        def quantise_w2(j):
+            w2_codes[j] = keep.tile([P, PASSES2 * P], U32, name=f"w2codes{j}", align_bytes=64)
+            w2_scale[j] = keep.tile([P, PASSES2 * P], U8, name=f"w2scale{j}", align_bytes=64)
+            nc.vector.quantize_mx(
+                out=w2_codes[j][:].bitcast(FP8X4),
+                scales=w2_scale[j][:],
+                in_=w2_woven[j][:].rearrange("p b c i -> p (b c i)"),
+            )
+
+        for j in range(4):
+            for h in range(HALVES):
+                first_product(j, h, 0)
+        for j in range(2):
+            for h in range(HALVES):
+                first_product(j, h, 1)
+        for j in range(2):
+            first_product(j, 0, 2)
+        for h in range(HALVES):
+            first_product(2, h, 1)
+        for j in range(2):
+            first_product(j, 1, 2)
+        read_heads(0)
+        for h in range(HALVES):
+            first_product(2, h, 2)
+        read_heads(1)
+        for h in range(HALVES):
+            first_product(3, h, 1)
+            first_product(3, h, 2)
+        read_heads(2)
+        for j in range(4, TILES):
+            for h in range(HALVES):
+                for a in range(PASSES1):
+                    first_product(j, h, a)
+            read_heads(j - 1)
+        read_heads(TILES - 1)
+        for j in range(TILES):
+            offset_plane(j)
+        round_w2(0)
+        weave_z(0)
+        quantise_z(0)
+        weave_z(1)
+        quantise_w2(0)
+        quantise_z(1)
+        round_w2(1)
+        quantise_w2(1)
+
+        y_sb = {}
+
+        def second_product(j):
+            e_bank = psum.tile([P, M], F32, name="bank")
+            for b in range(PASSES2):
+                cols = slice(b * P, (b + 1) * P)
+                nc.tensor.matmul_mx(
+                    out=e_bank[:],
+                    lhsT=w2_codes[j][:, cols].bitcast(FP8X4),
+                    lhsT_scale=w2_scale[j][:, cols],
+                    rhs=z_codes[b][:].bitcast(FP8X4),
+                    rhs_scale=z_scale[b][:],
+                    start=(b == 0),
+                    stop=(b == PASSES2 - 1),
+                )
+            ex = ring.tile([P, M], F32, name="ex")
+            nc.vector.tensor_tensor(ex[:], e_bank[:], x_sb[j][:], MULT)
+            y_sb[j] = ring.tile([P, M], F32, name="y_sb")
+            if j == 0:
+                nc.vector.tensor_tensor(y_sb[j][:], ex[:], prior_sb[j][:], ADD)
+                return
+            turned = psum.tile([P, M], F32, name="bank")
+            blocks = [slice(c * P, (c + 1) * P) for c in range(M // P)]
+            for term, source in enumerate((prior_sb[j], ex)):
+                for c, block in enumerate(blocks):
+                    nc.tensor.matmul(
+                        turned[:, block], source[:, block], ident[:], is_transpose=True,
+                        start=(term == 0 and c == 0), stop=(term == 1 and c == len(blocks) - 1),
+                    )
+            turned_sb = ring.tile([P, M], F32, name="turned_sb")
+            nc.scalar.copy(turned_sb[:], turned[:])
+            back = psum.tile([P, M], F32, name="bank")
+            for block in blocks:
+                nc.tensor.transpose(back[:, block], turned_sb[:, block], ident[:])
+            nc.scalar.copy(y_sb[j][:], back[:])
+
+        def file_scores(j):
+            page = pages[j % PAGES]
+            nc.vector.tensor_tensor(page[:].indirect(list3[:]), y_sb[j][:], wgo_sb[:], MULT)
+            nc.sync.dma_start(rows(out, j), page[:])
+
+        second_product(0)
+        for j in range(TILES):
+            if j + 1 < TILES:
+                second_product(j + 1)
+            if j + 2 < TILES:
+                round_w2(j + 2)
+            file_scores(j)
+            if j + 2 < TILES:
+                quantise_w2(j + 2)

@@ -26,6 +26,9 @@ PASSES2 = H // (P * PACK)
 TILES = H // P
 HALVES = S // N
 PAGES = 3
+DEAD = 32 - 4 * PASSES1
+SPAN = 100
+SLOT = 4 * T
 
 
 def tile_list_jewellery_drawer_appraisal_kernel(
@@ -40,79 +43,76 @@ def tile_list_jewellery_drawer_appraisal_kernel(
     with ExitStack() as ctx:
         keep = ctx.enter_context(tc.tile_pool(name="keep", bufs=1))
         ring = ctx.enter_context(tc.tile_pool(name="ring", bufs=2))
+        arena = ctx.enter_context(tc.tile_pool(name="arena", bufs=1))
         hpool = ctx.enter_context(tc.tile_pool(name="hpool", bufs=4))
         psum = ctx.enter_context(tc.psum_pool(name="psum", bufs=8))
 
         list1 = keep.tile([P, S // 16], U16, name="list1")
         list2 = keep.tile([P, M // 16], U16, name="list2")
         list3 = keep.tile([P, M // 16], U16, name="list3")
-        tscale = keep.tile([P, T], U8, name="tscale", align_bytes=64)
-        wscale_raw = keep.tile([P, PASSES1, H], U8, name="wscale_raw", align_bytes=64)
+        tscale = arena.tile([P, T], U8, name="tscale", align_bytes=64, offset=3 * SLOT)
+        wscale_raw = arena.tile([P, PASSES1, H], U8, name="wscale_raw", align_bytes=64, offset=6 * SLOT + T)
         vscale = [keep.tile([P, S], U8, name=f"vscale{a}", align_bytes=64) for a in range(PASSES1)]
-        pages = [keep.tile([P, T2], F32, name=f"page{g}") for g in range(PAGES)]
         metal_rows = keep.tile([P, P], F32, name="metal_rows")
         ident = keep.tile([P, P], F32, name="ident")
 
-        nc.vector.memset(tscale[:].bitcast(I32), 0)
         nc.vector.memset(wscale_raw[:].bitcast(I32), 0)
-        for a in range(1, PASSES1):
-            nc.vector.memset(vscale[a][:].bitcast(I32), 0)
-        for page in pages:
-            nc.vector.memset(page[:], 0.0)
+        for q in range(4):
+            engine = nc.vector if q < 2 else nc.gpsimd
+            engine.memset(tscale[32 * q : 32 * q + DEAD, :].bitcast(I32), 0)
+        for a in range(PASSES1):
+            nc.vector.memset(vscale[a][96:P, :].bitcast(I32), 0)
         nc.gpsimd.memset(metal_rows[:], 0.0)
+        for b in range(PASSES2):
+            nc.gpsimd.dma_start(
+                metal_rows[PACK * b : PACK * (b + 1), :].rearrange("i (u s) -> i u s", s=8),
+                metal.rearrange("(b u i s) -> b i u s", b=PASSES2, i=PACK, s=8)[b],
+            )
         make_identity(nc, ident[:])
-
         nc.sync.dma_start(list1[:], offs)
         for q in range(4):
             queue = nc.sync if q < 2 else nc.scalar
             queue.dma_start(
-                tscale[32 * q : 32 * q + 4 * PASSES1, :].bitcast(I32),
+                tscale[32 * q + DEAD : 32 * (q + 1), :].bitcast(I32),
                 tab_scales[:, 4 * q : 4 * q + 4, :].bitcast(I32),
             )
 
-        twords = [keep.tile([P, T], I32, name=f"twords{a}") for a in range(PASSES1)]
-        wwords_raw = keep.tile([P, PASSES1, H // 2], I32, name="wwords_raw")
+        for q in range(4):
+            nc.scalar.dma_start(
+                wscale_raw[32 * q : 32 * q + 4, :, :].bitcast(I32),
+                w4_scales[:, 4 * q : 4 * q + 4, :].rearrange("a r n -> r a n").bitcast(I32),
+            )
+        twords = [arena.tile([P, T], I32, name=f"twords{a}", offset=(0, 2, 3)[a] * SLOT) for a in range(PASSES1)]
+        wwords_raw = arena.tile([P, PASSES1, H // 2], I32, name="wwords_raw", offset=SLOT)
 
         def load_table(a):
             nc.sync.dma_start(twords[a][:], tab_words[a].rearrange("p t i -> p (t i)").bitcast(I32))
 
         load_table(0)
         nc.sync.dma_start(wwords_raw[:], w4_words.rearrange("a p n -> p a n").bitcast(I32))
-        for q in range(4):
-            nc.scalar.dma_start(
-                wscale_raw[32 * q : 32 * q + 4, :, :].bitcast(I32),
-                w4_scales[:, 4 * q : 4 * q + 4, :].rearrange("a r n -> r a n").bitcast(I32),
-            )
+
         load_table(1)
-        for b in range(PASSES2):
-            nc.scalar.dma_start(
-                metal_rows[PACK * b : PACK * (b + 1), :].rearrange("i (u s) -> i u s", s=8),
-                metal.rearrange("(b u i s) -> b i u s", b=PASSES2, i=PACK, s=8)[b],
-            )
+        picked = arena.tile([P, S], U8, name="picked", align_bytes=64, offset=6 * SLOT)
+        nc.vector.tensor_copy(picked[:], tscale[:].indirect(list1[:]))
+        for a in range(PASSES1):
+            first = DEAD + 4 * a
+            nc.scalar.dma_start(vscale[a][0:SPAN, :].bitcast(I32), picked[first : first + SPAN, :].bitcast(I32))
+        load_table(2)
         metal_bank = psum.tile([P, P], F32, name="bank")
         nc.tensor.transpose(metal_bank[:], metal_rows[:], ident[:])
         metal_sb = keep.tile([P, TILES], F32, name="metal_sb")
         nc.scalar.activation(metal_sb[:], metal_bank[:, 0:TILES], IDENTITY)
 
-        nc.vector.tensor_copy(vscale[0][:], tscale[:].indirect(list1[:]))
-        for a in range(1, PASSES1):
-            nc.scalar.dma_start(vscale[a][0:112, :].bitcast(I32), vscale[0][4 * a : 4 * a + 112, :].bitcast(I32))
-        load_table(2)
 
         nc.sync.dma_start(list2[:], offs2)
-        wgt_sb = keep.tile([P, M], F32, name="wgt_sb")
-        nc.sync.dma_start(wgt_sb[:], wgt)
-        w2_raw = [keep.tile([P, PACK, H], F32, name=f"w2raw{b}") for b in range(PASSES2)]
-        for j in range(TILES):
-            nc.sync.dma_start(w2_raw[j // PACK][:, j % PACK, :], rows(w2, j))
-        prior_sb = [keep.tile([P, M], F32, name=f"prior{j}") for j in range(TILES)]
-        wgo_sb = keep.tile([P, M], F32, name="wgo_sb")
         nc.sync.dma_start(list3[:], offs3)
-        nc.sync.dma_start(wgo_sb[:], wgo)
-        for j in range(TILES):
-            nc.sync.dma_start(prior_sb[j][:], rows(prior, j))
-
-        vwords = [[keep.tile([P, N], U32, name=f"vwords{a}_{h}", align_bytes=64) for h in range(HALVES)] for a in range(PASSES1)]
+        vwords = [
+            [
+                arena.tile([P, N], U32, name=f"vwords{a}_{h}", align_bytes=64, offset=(4, 5, 7)[a] * SLOT + h * 4 * N)
+                for h in range(HALVES)
+            ]
+            for a in range(PASSES1)
+        ]
 
         def gather_table(a):
             for h in range(HALVES):
@@ -122,21 +122,51 @@ def tile_list_jewellery_drawer_appraisal_kernel(
         wwords = [keep.tile([P, PASSES1, PACK, 2 * P], U8, name=f"wwords{b}", align_bytes=64) for b in range(PASSES2)]
         wscale = [keep.tile([P, PASSES1, PACK, P], U8, name=f"wscale{b}", align_bytes=64) for b in range(PASSES2)]
 
-        def deal_w4(b):
+        def deal_w4_words(b):
             nc.vector.tensor_copy(
-                wwords[b][:].bitcast(I32).rearrange("p a i (u w) -> p a i u w", w=4),
-                wwords_raw[:].rearrange("p a (b u i w) -> p b a i u w", b=PASSES2, i=PACK, w=4)[:, b],
+                wwords[b][:].bitcast(I32).rearrange("p a i (u w) -> p i a u w", w=4),
+                wwords_raw[:].rearrange("p a (b u i w) -> p b i a u w", b=PASSES2, i=PACK, w=4)[:, b],
             )
+
+        def deal_w4_scales(b):
             nc.vector.tensor_copy(
-                wscale[b][:].bitcast(I32).rearrange("p a i (u w) -> p a i u w", w=2),
-                wscale_raw[:].bitcast(I32).rearrange("p a (b u i w) -> p b a i u w", b=PASSES2, i=PACK, w=2)[:, b],
+                wscale[b][:].bitcast(I32).rearrange("p a i (u w) -> p i a u w", w=2),
+                wscale_raw[:].bitcast(I32).rearrange("p a (b u i w) -> p b i a u w", b=PASSES2, i=PACK, w=2)[:, b],
             )
 
         gather_table(0)
-        deal_w4(0)
-        deal_w4(1)
+        for b in range(PASSES2):
+            deal_w4_words(b)
+        for b in range(PASSES2):
+            deal_w4_scales(b)
         gather_table(1)
         gather_table(2)
+        pages = [keep.tile([P, T2], F32, name="page0")] + [
+            arena.tile([P, T2], F32, name=f"page{g}", offset=3 * SLOT + (g - 1) * 4 * T2) for g in range(1, PAGES)
+        ]
+        for page in pages:
+            nc.vector.memset(page[:], 0.0)
+
+        wgt_sb = arena.tile([P, M], F32, name="wgt_sb", offset=6 * SLOT)
+        nc.sync.dma_start(wgt_sb[:], wgt)
+        w2_raw = [
+            [arena.tile([P, PACK, N], F32, name=f"w2raw{c}_{b}", offset=((0, 1), (7, 4))[c][b] * SLOT) for b in range(PASSES2)]
+            for c in range(PASSES2)
+        ]
+        prior_sb = [
+            arena.tile([P, M], F32, name=f"prior{j}", offset=(2 + 3 * (j // PACK)) * SLOT + (j % PACK) * 4 * M)
+            for j in range(TILES)
+        ]
+        wgo_sb = arena.tile([P, M], F32, name="wgo_sb", offset=6 * SLOT + T)
+        nc.sync.dma_start(wgo_sb[:], wgo)
+
+        def load_second_stage(c):
+            for j in range(TILES):
+                nc.sync.dma_start(w2_raw[c][j // PACK][:, j % PACK, :], rows(w2, j)[:, :, c * N : (c + 1) * N])
+            for j in range(c * PACK, (c + 1) * PACK):
+                nc.sync.dma_start(prior_sb[j][:], rows(prior, j))
+
+        load_second_stage(0)
 
         h_sb = {}
         h_bank = {}
@@ -175,7 +205,10 @@ def tile_list_jewellery_drawer_appraisal_kernel(
 
         def weave_z(b):
             z_woven[b] = ring.tile([P, M, PACK], BF16, name="z_woven", align_bytes=64)
-            nc.vector.tensor_copy(z_woven[b][:], z_planes[b][:].rearrange("p i m -> p m i"))
+            nc.vector.tensor_copy(
+                z_woven[b][:].rearrange("p (c r) i -> p c i r", r=4),
+                z_planes[b][:].rearrange("p i (c r) -> p c i r", r=4),
+            )
 
         def quantise_z(b):
             nc.vector.quantize_mx(
@@ -188,48 +221,37 @@ def tile_list_jewellery_drawer_appraisal_kernel(
 
         def round_w2(j):
             bn, i_n = divmod(j, PACK)
-            w2_woven[j] = ring.tile([P, PASSES2, P, PACK], BF16, name="w2_woven", align_bytes=64)
+            w2_woven[j] = keep.tile([P, PASSES2, P, PACK], BF16, name="w2_woven", align_bytes=64)
             for b in range(PASSES2):
                 nc.scalar.copy(
-                    w2_woven[j][:, b].rearrange("p (u s) i -> p u s i", s=8),
-                    w2_raw[b][:].rearrange("p i (c u n s) -> p c n u s i", c=PASSES2, n=PACK, s=8)[:, bn, i_n],
+                    w2_woven[j][:, b].rearrange("p (u s r) i -> p u s i r", s=2, r=4),
+                    w2_raw[bn][b][:].rearrange("p i (u n s r) -> p n u s i r", n=PACK, s=2, r=4)[:, i_n],
                 )
 
         def quantise_w2(j):
-            w2_codes[j] = keep.tile([P, PASSES2 * P], U32, name=f"w2codes{j}", align_bytes=64)
-            w2_scale[j] = keep.tile([P, PASSES2 * P], U8, name=f"w2scale{j}", align_bytes=64)
+            w2_codes[j] = ring.tile([P, PASSES2 * P], U32, name="w2codes", align_bytes=64)
+            w2_scale[j] = ring.tile([P, PASSES2 * P], U8, name="w2scale", align_bytes=64)
             nc.vector.quantize_mx(
                 out=w2_codes[j][:].bitcast(FP8X4),
                 scales=w2_scale[j][:],
                 in_=w2_woven[j][:].rearrange("p b c i -> p (b c i)"),
             )
 
-        for j in range(4):
-            for h in range(HALVES):
-                first_product(j, h, 0)
-        for j in range(2):
-            for h in range(HALVES):
-                first_product(j, h, 1)
-        for j in range(2):
-            first_product(j, 0, 2)
+        for a, early in ((0, 3), (1, 2)):
+            for j in range(early):
+                for h in range(HALVES):
+                    first_product(j, h, a)
         for h in range(HALVES):
-            first_product(2, h, 1)
-        for j in range(2):
-            first_product(j, 1, 2)
+            for j in range(2):
+                first_product(j, h, 2)
         read_heads(0)
-        for h in range(HALVES):
-            first_product(2, h, 2)
-        read_heads(1)
-        for h in range(HALVES):
-            first_product(3, h, 1)
-            first_product(3, h, 2)
-        read_heads(2)
-        for j in range(4, TILES):
+        for j in range(2, TILES):
             for h in range(HALVES):
-                for a in range(PASSES1):
+                for a in range(1 if j == 2 else 0, PASSES1):
                     first_product(j, h, a)
             read_heads(j - 1)
         read_heads(TILES - 1)
+        load_second_stage(1)
         for j in range(TILES):
             offset_plane(j)
         round_w2(0)
@@ -241,6 +263,7 @@ def tile_list_jewellery_drawer_appraisal_kernel(
         round_w2(1)
         quantise_w2(1)
 
+        ex = {}
         y_sb = {}
 
         def second_product(j):
@@ -256,26 +279,12 @@ def tile_list_jewellery_drawer_appraisal_kernel(
                     start=(b == 0),
                     stop=(b == PASSES2 - 1),
                 )
-            ex = ring.tile([P, M], F32, name="ex")
-            nc.vector.tensor_tensor(ex[:], e_bank[:], x_sb[j][:], MULT)
+            ex[j] = ring.tile([P, M], F32, name="ex")
+            nc.vector.tensor_tensor(ex[j][:], e_bank[:], x_sb[j][:], MULT)
+
+        def add_prior(j):
             y_sb[j] = ring.tile([P, M], F32, name="y_sb")
-            if j == 0:
-                nc.vector.tensor_tensor(y_sb[j][:], ex[:], prior_sb[j][:], ADD)
-                return
-            turned = psum.tile([P, M], F32, name="bank")
-            blocks = [slice(c * P, (c + 1) * P) for c in range(M // P)]
-            for term, source in enumerate((prior_sb[j], ex)):
-                for c, block in enumerate(blocks):
-                    nc.tensor.matmul(
-                        turned[:, block], source[:, block], ident[:], is_transpose=True,
-                        start=(term == 0 and c == 0), stop=(term == 1 and c == len(blocks) - 1),
-                    )
-            turned_sb = ring.tile([P, M], F32, name="turned_sb")
-            nc.scalar.copy(turned_sb[:], turned[:])
-            back = psum.tile([P, M], F32, name="bank")
-            for block in blocks:
-                nc.tensor.transpose(back[:, block], turned_sb[:, block], ident[:])
-            nc.scalar.copy(y_sb[j][:], back[:])
+            nc.vector.tensor_tensor(y_sb[j][:], ex[j][:], prior_sb[j][:], ADD)
 
         def file_scores(j):
             page = pages[j % PAGES]
@@ -284,10 +293,10 @@ def tile_list_jewellery_drawer_appraisal_kernel(
 
         second_product(0)
         for j in range(TILES):
-            if j + 1 < TILES:
-                second_product(j + 1)
             if j + 2 < TILES:
                 round_w2(j + 2)
-            file_scores(j)
-            if j + 2 < TILES:
                 quantise_w2(j + 2)
+            add_prior(j)
+            if j + 1 < TILES:
+                second_product(j + 1)
+            file_scores(j)

@@ -26,6 +26,8 @@ PASSES2 = H // (P * PACK)
 TILES = H // P
 HALVES = S // N
 PAGES = 3
+BANKS = 8
+STAGES = 4
 DEAD = 32 - 4 * PASSES1
 SPAN = 100
 SLOT = 4 * T
@@ -45,7 +47,8 @@ def tile_list_jewellery_drawer_appraisal_kernel(
         ring = ctx.enter_context(tc.tile_pool(name="ring", bufs=2))
         arena = ctx.enter_context(tc.tile_pool(name="arena", bufs=1))
         hpool = ctx.enter_context(tc.tile_pool(name="hpool", bufs=4))
-        psum = ctx.enter_context(tc.psum_pool(name="psum", bufs=8))
+        psum = ctx.enter_context(tc.psum_pool(name="psum", bufs=1))
+        banks = [psum.tile([P, N], F32, name=f"bank{g}") for g in range(BANKS)]
 
         list1 = keep.tile([P, S // 16], U16, name="list1")
         list2 = keep.tile([P, M // 16], U16, name="list2")
@@ -98,8 +101,8 @@ def tile_list_jewellery_drawer_appraisal_kernel(
             first = DEAD + 4 * a
             nc.scalar.dma_start(vscale[a][0:SPAN, :].bitcast(I32), picked[first : first + SPAN, :].bitcast(I32))
         load_table(2)
-        metal_bank = psum.tile([P, P], F32, name="bank")
-        nc.tensor.transpose(metal_bank[:], metal_rows[:], ident[:])
+        metal_bank = banks[BANKS - 1]
+        nc.tensor.transpose(metal_bank[:, 0:P], metal_rows[:], ident[:])
         metal_sb = keep.tile([P, TILES], F32, name="metal_sb")
         nc.scalar.activation(metal_sb[:], metal_bank[:, 0:TILES], IDENTITY)
 
@@ -174,7 +177,7 @@ def tile_list_jewellery_drawer_appraisal_kernel(
         def first_product(j, h, a):
             b, i = divmod(j, PACK)
             if a == 0:
-                h_bank[j, h] = psum.tile([P, N], F32, name="bank")
+                h_bank[j, h] = banks[(HALVES * j + h) % BANKS]
             nc.tensor.matmul_mx(
                 out=h_bank[j, h][:],
                 lhsT=wwords[b][:, a, i, :].bitcast(FP4X4),
@@ -215,13 +218,14 @@ def tile_list_jewellery_drawer_appraisal_kernel(
                 out=z_codes[b][:].bitcast(FP8X4), scales=z_scale[b][:], in_=z_woven[b][:].rearrange("p m i -> p (m i)")
             )
 
+        stage = [keep.tile([P, M], F32, name=f"stage{g}", align_bytes=64) for g in range(STAGES)]
         w2_woven = {}
         w2_codes = {}
         w2_scale = {}
 
         def round_w2(j):
             bn, i_n = divmod(j, PACK)
-            w2_woven[j] = keep.tile([P, PASSES2, P, PACK], BF16, name="w2_woven", align_bytes=64)
+            w2_woven[j] = stage[j % STAGES][:].bitcast(BF16).rearrange("p (b c i) -> p b c i", b=PASSES2, i=PACK)
             for b in range(PASSES2):
                 nc.scalar.copy(
                     w2_woven[j][:, b].rearrange("p (u s r) i -> p u s i r", s=2, r=4),
@@ -229,12 +233,12 @@ def tile_list_jewellery_drawer_appraisal_kernel(
                 )
 
         def quantise_w2(j):
-            w2_codes[j] = ring.tile([P, PASSES2 * P], U32, name="w2codes", align_bytes=64)
-            w2_scale[j] = ring.tile([P, PASSES2 * P], U8, name="w2scale", align_bytes=64)
+            w2_codes[j] = keep.tile([P, PASSES2 * P], U32, name=f"w2codes{j}", align_bytes=64)
+            w2_scale[j] = keep.tile([P, PASSES2 * P], U8, name=f"w2scale{j}", align_bytes=64)
             nc.vector.quantize_mx(
                 out=w2_codes[j][:].bitcast(FP8X4),
                 scales=w2_scale[j][:],
-                in_=w2_woven[j][:].rearrange("p b c i -> p (b c i)"),
+                in_=stage[j % STAGES][:].bitcast(BF16),
             )
 
         for a, early in ((0, 3), (1, 2)):
@@ -260,14 +264,15 @@ def tile_list_jewellery_drawer_appraisal_kernel(
         weave_z(1)
         quantise_w2(0)
         quantise_z(1)
-        round_w2(1)
-        quantise_w2(1)
+        for j in range(1, STAGES):
+            round_w2(j)
+            quantise_w2(j)
 
-        ex = {}
-        y_sb = {}
+        scores = [keep.tile([P, M], F32, name=f"scores{g}") for g in range(STAGES)]
+        blocks = [slice(c * P, (c + 1) * P) for c in range(M // P)]
 
         def second_product(j):
-            e_bank = psum.tile([P, M], F32, name="bank")
+            e_bank = banks[j % 2]
             for b in range(PASSES2):
                 cols = slice(b * P, (b + 1) * P)
                 nc.tensor.matmul_mx(
@@ -279,24 +284,37 @@ def tile_list_jewellery_drawer_appraisal_kernel(
                     start=(b == 0),
                     stop=(b == PASSES2 - 1),
                 )
-            ex[j] = ring.tile([P, M], F32, name="ex")
-            nc.vector.tensor_tensor(ex[j][:], e_bank[:], x_sb[j][:], MULT)
-
-        def add_prior(j):
-            y_sb[j] = ring.tile([P, M], F32, name="y_sb")
-            nc.vector.tensor_tensor(y_sb[j][:], ex[j][:], prior_sb[j][:], ADD)
+            ex = stage[0] if j == 0 else scores[(j + 1) % STAGES]
+            y_sb = scores[j % STAGES]
+            nc.vector.tensor_tensor(ex[:], e_bank[:], x_sb[j][:], MULT)
+            if j == 0:
+                nc.vector.tensor_tensor(y_sb[:], ex[:], prior_sb[j][:], ADD)
+                return
+            turned = banks[2 + j % 3]
+            for term, source in enumerate((prior_sb[j], ex)):
+                for c, block in enumerate(blocks):
+                    nc.tensor.matmul(
+                        turned[:, block], source[:, block], ident[:], is_transpose=True,
+                        start=(term == 0 and c == 0), stop=(term == 1 and c == len(blocks) - 1),
+                    )
+            turned_sb = stage[j % STAGES]
+            nc.scalar.copy(turned_sb[:], turned[:])
+            back = banks[5 + j % 3]
+            for block in blocks:
+                nc.tensor.transpose(back[:, block], turned_sb[:, block], ident[:])
+            nc.scalar.copy(y_sb[:], back[:])
 
         def file_scores(j):
             page = pages[j % PAGES]
-            nc.vector.tensor_tensor(page[:].indirect(list3[:]), y_sb[j][:], wgo_sb[:], MULT)
+            nc.vector.tensor_tensor(page[:].indirect(list3[:]), scores[j % STAGES][:], wgo_sb[:], MULT)
             nc.sync.dma_start(rows(out, j), page[:])
 
         second_product(0)
+        second_product(1)
         for j in range(TILES):
             if j + 2 < TILES:
-                round_w2(j + 2)
-                quantise_w2(j + 2)
-            add_prior(j)
-            if j + 1 < TILES:
-                second_product(j + 1)
+                second_product(j + 2)
             file_scores(j)
+            if j + STAGES < TILES:
+                round_w2(j + STAGES)
+                quantise_w2(j + STAGES)

from contextlib import ExitStack

import concourse.mybir as mybir
from concourse.masks import make_identity

K, H, T, S, M, T2 = 1536, 1024, 2048, 1024, 512, 1024
FLOPS = 2 * K * H * S + 2 * H * H * M

F32 = mybir.dt.float32
BF16 = mybir.dt.bfloat16
I32 = mybir.dt.int32
U32 = mybir.dt.uint32
U16 = mybir.dt.uint16
U8 = mybir.dt.uint8
FP8X4 = mybir.dt.float8_e4m3fn_x4
FP4X4 = mybir.dt.float4_e2m1fn_x4
MULT = mybir.AluOpType.mult
ADD = mybir.AluOpType.add
IDENTITY = mybir.ActivationFunctionType.Identity

P = 128
PACK = 4
N = 512
PASSES1 = K // (P * PACK)
PASSES2 = H // (P * PACK)
TILES = H // P
HALVES = S // N
PAGES = 3
BANKS = 8
STAGES = 4
DEAD = 32 - 4 * PASSES1
SPAN = 100
SLOT = 4 * T


def tile_list_jewellery_drawer_appraisal_kernel(
    tc, tab_words, tab_scales, w4_words, w4_scales, w2, metal, prior, wgt, wgo, offs, offs2, offs3, out
):
    nc = tc.nc

    def rows(dram, j):
        b, i = divmod(j, PACK)
        return dram.rearrange("(b u i s) c -> b i u s c", b=PASSES2, i=PACK, s=8)[b, i]

    with ExitStack() as ctx:
        keep = ctx.enter_context(tc.tile_pool(name="keep", bufs=1))
        ring = ctx.enter_context(tc.tile_pool(name="ring", bufs=2))
        arena = ctx.enter_context(tc.tile_pool(name="arena", bufs=1))
        hpool = ctx.enter_context(tc.tile_pool(name="hpool", bufs=4))
        psum = ctx.enter_context(tc.psum_pool(name="psum", bufs=1))
        banks = [psum.tile([P, N], F32, name=f"bank{g}") for g in range(BANKS)]

        list1 = keep.tile([P, S // 16], U16, name="list1")
        list2 = keep.tile([P, M // 16], U16, name="list2")
        list3 = keep.tile([P, M // 16], U16, name="list3")
        tscale = arena.tile([P, T], U8, name="tscale", align_bytes=64, offset=3 * SLOT)
        wscale_raw = arena.tile([P, PASSES1, H], U8, name="wscale_raw", align_bytes=64, offset=6 * SLOT + T)
        vscale = [keep.tile([P, S], U8, name=f"vscale{a}", align_bytes=64) for a in range(PASSES1)]
        metal_rows = keep.tile([P, P], F32, name="metal_rows")
        ident = keep.tile([P, P], F32, name="ident")

        nc.vector.memset(wscale_raw[:].bitcast(I32), 0)
        for q in range(4):
            engine = nc.vector if q < 2 else nc.gpsimd
            engine.memset(tscale[32 * q : 32 * q + DEAD, :].bitcast(I32), 0)
        for a in range(PASSES1):
            nc.vector.memset(vscale[a][96:P, :].bitcast(I32), 0)
        nc.gpsimd.memset(metal_rows[:], 0.0)
        for b in range(PASSES2):
            nc.gpsimd.dma_start(
                metal_rows[PACK * b : PACK * (b + 1), :].rearrange("i (u s) -> i u s", s=8),
                metal.rearrange("(b u i s) -> b i u s", b=PASSES2, i=PACK, s=8)[b],
            )
        make_identity(nc, ident[:])
        nc.sync.dma_start(list1[:], offs)
        for q in range(4):
            queue = nc.sync if q < 2 else nc.scalar
            queue.dma_start(
                tscale[32 * q + DEAD : 32 * (q + 1), :].bitcast(I32),
                tab_scales[:, 4 * q : 4 * q + 4, :].bitcast(I32),
            )

        for q in range(4):
            nc.scalar.dma_start(
                wscale_raw[32 * q : 32 * q + 4, :, :].bitcast(I32),
                w4_scales[:, 4 * q : 4 * q + 4, :].rearrange("a r n -> r a n").bitcast(I32),
            )
        twords = [arena.tile([P, T], I32, name=f"twords{a}", offset=(0, 2, 3)[a] * SLOT) for a in range(PASSES1)]
        wwords_raw = arena.tile([P, PASSES1, H // 2], I32, name="wwords_raw", offset=SLOT)

        def load_table(a):
            nc.sync.dma_start(twords[a][:], tab_words[a].rearrange("p t i -> p (t i)").bitcast(I32))

        load_table(0)
        nc.sync.dma_start(wwords_raw[:], w4_words.rearrange("a p n -> p a n").bitcast(I32))

        load_table(1)
        picked = arena.tile([P, S], U8, name="picked", align_bytes=64, offset=6 * SLOT)
        nc.vector.tensor_copy(picked[:], tscale[:].indirect(list1[:]))
        for a in range(PASSES1):
            first = DEAD + 4 * a
            nc.scalar.dma_start(vscale[a][0:SPAN, :].bitcast(I32), picked[first : first + SPAN, :].bitcast(I32))
        load_table(2)
        metal_bank = banks[BANKS - 1]
        nc.tensor.transpose(metal_bank[:, 0:P], metal_rows[:], ident[:])
        metal_sb = keep.tile([P, TILES], F32, name="metal_sb")
        nc.scalar.activation(metal_sb[:], metal_bank[:, 0:TILES], IDENTITY)


        nc.sync.dma_start(list2[:], offs2)
        nc.sync.dma_start(list3[:], offs3)
        vwords = [
            [
                arena.tile([P, N], U32, name=f"vwords{a}_{h}", align_bytes=64, offset=(4, 5, 7)[a] * SLOT + h * 4 * N)
                for h in range(HALVES)
            ]
            for a in range(PASSES1)
        ]

        def gather_table(a):
            for h in range(HALVES):
                cols = list1[:, h * (N // 16) : (h + 1) * (N // 16)]
                nc.vector.tensor_copy(vwords[a][h][:], twords[a][:].bitcast(U32).indirect(cols))

        wwords = [keep.tile([P, PASSES1, PACK, 2 * P], U8, name=f"wwords{b}", align_bytes=64) for b in range(PASSES2)]
        wscale = [keep.tile([P, PASSES1, PACK, P], U8, name=f"wscale{b}", align_bytes=64) for b in range(PASSES2)]

        def deal_w4_words(b):
            nc.vector.tensor_copy(
                wwords[b][:].bitcast(I32).rearrange("p a i (u w) -> p i a u w", w=4),
                wwords_raw[:].rearrange("p a (b u i w) -> p b i a u w", b=PASSES2, i=PACK, w=4)[:, b],
            )

        def deal_w4_scales(b):
            nc.vector.tensor_copy(
                wscale[b][:].bitcast(I32).rearrange("p a i (u w) -> p i a u w", w=2),
                wscale_raw[:].bitcast(I32).rearrange("p a (b u i w) -> p b i a u w", b=PASSES2, i=PACK, w=2)[:, b],
            )

        gather_table(0)
        for b in range(PASSES2):
            deal_w4_words(b)
        for b in range(PASSES2):
            deal_w4_scales(b)
        gather_table(1)
        gather_table(2)
        pages = [keep.tile([P, T2], F32, name="page0")] + [
            arena.tile([P, T2], F32, name=f"page{g}", offset=3 * SLOT + (g - 1) * 4 * T2) for g in range(1, PAGES)
        ]
        for page in pages:
            nc.vector.memset(page[:], 0.0)

        wgt_sb = arena.tile([P, M], F32, name="wgt_sb", offset=6 * SLOT)
        nc.sync.dma_start(wgt_sb[:], wgt)
        w2_raw = [
            [arena.tile([P, PACK, N], F32, name=f"w2raw{c}_{b}", offset=((0, 1), (7, 4))[c][b] * SLOT) for b in range(PASSES2)]
            for c in range(PASSES2)
        ]
        prior_sb = [
            arena.tile([P, M], F32, name=f"prior{j}", offset=(2 + 3 * (j // PACK)) * SLOT + (j % PACK) * 4 * M)
            for j in range(TILES)
        ]
        wgo_sb = arena.tile([P, M], F32, name="wgo_sb", offset=6 * SLOT + T)
        nc.sync.dma_start(wgo_sb[:], wgo)

        def load_second_stage(c):
            for j in range(TILES):
                nc.sync.dma_start(w2_raw[c][j // PACK][:, j % PACK, :], rows(w2, j)[:, :, c * N : (c + 1) * N])
            for j in range(c * PACK, (c + 1) * PACK):
                nc.sync.dma_start(prior_sb[j][:], rows(prior, j))

        load_second_stage(0)

        h_sb = {}
        h_bank = {}

        def first_product(j, h, a):
            b, i = divmod(j, PACK)
            if a == 0:
                h_bank[j, h] = banks[(HALVES * j + h) % BANKS]
            nc.tensor.matmul_mx(
                out=h_bank[j, h][:],
                lhsT=wwords[b][:, a, i, :].bitcast(FP4X4),
                lhsT_scale=wscale[b][:, a, i, :],
                rhs=vwords[a][h][:].bitcast(FP8X4),
                rhs_scale=vscale[a][:, h * N : (h + 1) * N],
                start=(a == 0),
                stop=(a == PASSES1 - 1),
            )
            if a == PASSES1 - 1:
                if h == 0:
                    h_sb[j] = hpool.tile([P, S], F32, name="h_sb")
                nc.scalar.copy(h_sb[j][:, h * N : (h + 1) * N], h_bank[j, h][:])

        x_sb = [keep.tile([P, M], F32, name=f"x{j}") for j in range(TILES)]
        z_planes = [ring.tile([P, PACK, M], BF16, name="z_planes") for b in range(PASSES2)]
        z_codes = [keep.tile([P, M], U32, name=f"zcodes{b}", align_bytes=64) for b in range(PASSES2)]
        z_scale = [keep.tile([P, M], U8, name=f"zscale{b}", align_bytes=64) for b in range(PASSES2)]

        def read_heads(j):
            nc.vector.tensor_tensor(x_sb[j][:], h_sb[j][:].indirect(list2[:]), wgt_sb[:], MULT)

        def offset_plane(j):
            b, i = divmod(j, PACK)
            nc.scalar.activation(z_planes[b][:, i, :], x_sb[j][:], IDENTITY, bias=metal_sb[:, j : j + 1])

        z_woven = {}

        def weave_z(b):
            z_woven[b] = ring.tile([P, M, PACK], BF16, name="z_woven", align_bytes=64)
            nc.vector.tensor_copy(
                z_woven[b][:].rearrange("p (c r) i -> p c i r", r=4),
                z_planes[b][:].rearrange("p i (c r) -> p c i r", r=4),
            )

        def quantise_z(b):
            nc.vector.quantize_mx(
                out=z_codes[b][:].bitcast(FP8X4), scales=z_scale[b][:], in_=z_woven[b][:].rearrange("p m i -> p (m i)")
            )

        stage = [keep.tile([P, M], F32, name=f"stage{g}", align_bytes=64) for g in range(STAGES)]
        w2_woven = {}
        w2_codes = {}
        w2_scale = {}

        def round_w2(j):
            bn, i_n = divmod(j, PACK)
            w2_woven[j] = stage[j % STAGES][:].bitcast(BF16).rearrange("p (b c i) -> p b c i", b=PASSES2, i=PACK)
            for b in range(PASSES2):
                nc.scalar.copy(
                    w2_woven[j][:, b].rearrange("p (u s r) i -> p u s i r", s=2, r=4),
                    w2_raw[bn][b][:].rearrange("p i (u n s r) -> p n u s i r", n=PACK, s=2, r=4)[:, i_n],
                )

        def quantise_w2(j):
            w2_codes[j] = keep.tile([P, PASSES2 * P], U32, name=f"w2codes{j}", align_bytes=64)
            w2_scale[j] = keep.tile([P, PASSES2 * P], U8, name=f"w2scale{j}", align_bytes=64)
            nc.vector.quantize_mx(
                out=w2_codes[j][:].bitcast(FP8X4),
                scales=w2_scale[j][:],
                in_=stage[j % STAGES][:].bitcast(BF16),
            )

        for a, early in ((0, 3), (1, 2)):
            for j in range(early):
                for h in range(HALVES):
                    first_product(j, h, a)
        for h in range(HALVES):
            for j in range(2):
                first_product(j, h, 2)
        read_heads(0)
        for j in range(2, TILES):
            for h in range(HALVES):
                for a in range(1 if j == 2 else 0, PASSES1):
                    first_product(j, h, a)
            read_heads(j - 1)
        read_heads(TILES - 1)
        load_second_stage(1)
        for j in range(TILES):
            offset_plane(j)
        round_w2(0)
        weave_z(0)
        quantise_z(0)
        weave_z(1)
        quantise_w2(0)
        quantise_z(1)
        for j in range(1, STAGES):
            round_w2(j)
            quantise_w2(j)

        scores = [keep.tile([P, M], F32, name=f"scores{g}") for g in range(STAGES)]
        blocks = [slice(c * P, (c + 1) * P) for c in range(M // P)]

        def second_product(j):
            e_bank = banks[j % 2]
            for b in range(PASSES2):
                cols = slice(b * P, (b + 1) * P)
                nc.tensor.matmul_mx(
                    out=e_bank[:],
                    lhsT=w2_codes[j][:, cols].bitcast(FP8X4),
                    lhsT_scale=w2_scale[j][:, cols],
                    rhs=z_codes[b][:].bitcast(FP8X4),
                    rhs_scale=z_scale[b][:],
                    start=(b == 0),
                    stop=(b == PASSES2 - 1),
                )
            ex = stage[0] if j == 0 else scores[(j + 1) % STAGES]
            y_sb = scores[j % STAGES]
            nc.vector.tensor_tensor(ex[:], e_bank[:], x_sb[j][:], MULT)
            if j == 0:
                nc.vector.tensor_tensor(y_sb[:], ex[:], prior_sb[j][:], ADD)
                return
            turned = banks[2 + j % 3]
            for term, source in enumerate((prior_sb[j], ex)):
                for c, block in enumerate(blocks):
                    nc.tensor.matmul(
                        turned[:, block], source[:, block], ident[:], is_transpose=True,
                        start=(term == 0 and c == 0), stop=(term == 1 and c == len(blocks) - 1),
                    )
            turned_sb = stage[j % STAGES]
            nc.scalar.copy(turned_sb[:], turned[:])
            back = banks[5 + j % 3]
            for block in blocks:
                nc.tensor.transpose(back[:, block], turned_sb[:, block], ident[:])
            nc.scalar.copy(y_sb[:], back[:])

        def file_scores(j):
            page = pages[j % PAGES]
            nc.vector.tensor_tensor(page[:].indirect(list3[:]), scores[j % STAGES][:], wgo_sb[:], MULT)
            nc.sync.dma_start(rows(out, j), page[:])

        second_product(0)
        second_product(1)
        for j in range(TILES):
            if j + 2 < TILES:
                second_product(j + 2)
            file_scores(j)
            if j + STAGES < TILES:
                round_w2(j + STAGES)
                quantise_w2(j + STAGES)
